import numpy as np
import ml_dtypes


def mxq(x, axis, fmt="e4m3"):
    dtype, down = {"e4m3": (ml_dtypes.float8_e4m3fn, 7), "e5m2": (ml_dtypes.float8_e5m2, 14)}[fmt]
    v = np.moveaxis(np.asarray(x, np.float32).astype(ml_dtypes.bfloat16).astype(np.float64), axis, -1)
    blocks = v.reshape(v.shape[:-1] + (-1, 32))
    amax = np.abs(blocks).max(-1, keepdims=True)
    byte = np.maximum(np.where(amax > 0, np.frexp(amax)[1] - 1 + 127, 0) - down, 1)
    scale = np.exp2(byte - 127.0)
    codes = (blocks / scale).astype(np.float32).astype(dtype).astype(np.float64)
    return np.moveaxis((codes * scale).reshape(v.shape), -1, axis)


WIDE = False


def mx_kscale(k):
    if not WIDE:
        return np.ones(k)
    levels = np.array([10, -10, 5, -5, 0])
    if k % 512:
        return np.exp2(np.random.permutation(np.resize(levels, k // 32))).repeat(32)
    a = np.empty((k // 512, 16))
    for p in range(k // 512):
        a[p, :8] = np.random.permutation(np.resize(levels, 8))
        for g in range(8):
            far = levels[np.abs(levels - a[p, g]) >= 10]
            a[p, g + 8] = far[np.random.randint(len(far))]
    return np.exp2(a.ravel()).repeat(32)


def f64(x):
    return np.asarray(x).astype(np.float64)


def striped(idx):
    return np.tile(idx.reshape(-1, 16).T, (8, 1)).astype(np.uint16)


def unstriped(offs):
    return offs[:16].T.reshape(-1).astype(np.int64)


def striped8(idx):
    return np.concatenate([x.reshape(-1, 16).T for x in idx]).astype(np.uint16)


def runs(offs, k):
    lists = np.stack([offs[16 * r : 16 * r + 16].T.reshape(-1) for r in range(8)]).astype(np.int64)
    return lists[np.arange(k) % 512 // 64]


def pack_weight(w):
    k, n = w.shape
    w = f64(np.asarray(w, np.float32).astype(ml_dtypes.bfloat16)).reshape(k // 32, 32, n)
    amax = np.abs(w).max(1)
    byte = np.clip(np.where(amax > 0, np.frexp(amax)[1] - 1 + 127 - 7, 1), 1, 254)
    scaled = (w * np.exp2(127.0 - byte)[:, None, :]).reshape(k, n).astype(np.float32)
    words = np.ascontiguousarray(scaled.reshape(k // 512, 128, 4, n).transpose(0, 1, 3, 2)).astype(ml_dtypes.float8_e4m3fn).view(np.uint8)
    return words, np.ascontiguousarray(byte.astype(np.uint8).reshape(k // 512, 16, n))


def unpack_weight(words, scales):
    g, p, n, _ = words.shape
    vals = np.ascontiguousarray(words).view(ml_dtypes.float8_e4m3fn).astype(np.float64) * np.repeat(np.exp2(scales.astype(np.float64) - 127.0), 8, axis=1)[..., None]
    return vals.transpose(0, 1, 3, 2).reshape(g * 512, n)


K, T, S, V, H = 512, 2048, 512, 512, 512


def setup_inputs():
    n = np.random.standard_normal
    s = mx_kscale(K)[:, None]
    u = mx_kscale(S)
    packed_xT = pack_weight(n((K, T)) * s)
    return {
        "x_words": packed_xT[0],
        "x_scales": packed_xT[1],
        "w1": (n((K, H)) / np.sqrt(K) / s).astype(np.float32),
        "w2": (n((K, H)) / np.sqrt(K) / s).astype(np.float32),
        "ga": (np.random.uniform(0.5, 1.5, (H, 1)) * u[:, None]).astype(np.float32),
        "gb": (np.random.uniform(0.5, 1.5, (H, 1)) / u[:, None]).astype(np.float32),
        "offs": striped(np.random.permutation(T)[:S]),
        "two": striped(np.random.permutation(T)[:V]),
        "n1": striped8(np.stack([np.random.permutation(S) for _ in range(8)])),
        "n2": striped8(np.stack([np.random.permutation(S) for _ in range(8)])),
        "n3": striped8(np.stack([np.random.permutation(V) for _ in range(8)])),
        "n4": striped8(np.stack([np.random.permutation(V) for _ in range(8)])),
        "n5": striped8(np.stack([np.random.permutation(V) for _ in range(8)])),
        "n6": striped8(np.stack([np.random.permutation(V) for _ in range(8)])),
    }


def reference(x_words, x_scales, w1, w2, ga, gb, offs, two, n1, n2, n3, n4, n5, n6):
    xq = unpack_weight(x_words, x_scales)[:, unstriped(offs)]
    a = mxq(f64(w1), 0, "e4m3").T @ xq
    z = f64(ga) * (a * (a[np.arange(H)[:, None], runs(n1, H)] - (a[np.arange(H)[:, None], runs(n2, H)])))
    x_two = unpack_weight(x_words, x_scales)[:, unstriped(two)]
    b = mxq(f64(w2), 0, "e4m3").T @ x_two
    z2 = f64(gb) * ((b * (b[np.arange(H)[:, None], runs(n3, H)])) * (np.tanh(b[np.arange(H)[:, None], runs(n4, H)])))
    s = 0.0625 * ((mxq(z, 0, "e4m3").T @ mxq(z2, 0, "e4m3")))
    ex = np.exp(0.5 * s)
    return (2.0 * ex) / (ex + ex[np.arange(S)[:, None], runs(n5, S)] + ex[np.arange(S)[:, None], runs(n6, S)])

@@ -1,0 +1,203 @@
+from contextlib import ExitStack
+
+import concourse.mybir as mybir
+
+K, T, S, V, H = 512, 2048, 512, 512, 512
+FLOPS = 2 * K * H * S + 2 * K * H * V + 2 * H * S * V
+
+F32 = mybir.dt.float32
+BF16 = mybir.dt.bfloat16
+I32 = mybir.dt.int32
+U32 = mybir.dt.uint32
+U16 = mybir.dt.uint16
+U8 = mybir.dt.uint8
+FP8X4 = mybir.dt.float8_e4m3fn_x4
+ACT = mybir.ActivationFunctionType
+ALU = mybir.AluOpType
+
+P = 128
+PACK = 4
+N = 512
+
+
+def tile_picked_kqwindcubeshare_none_p_kernel(
+    tc, x_words, x_scales, w1, w2, ga, gb, offs, two, n1, n2, n3, n4, n5, n6, out
+):
+    nc = tc.nc
+    with ExitStack() as ctx:
+        lists = ctx.enter_context(tc.tile_pool(name="lists", bufs=1))
+        keep = ctx.enter_context(tc.tile_pool(name="keep", bufs=1))
+        ring = ctx.enter_context(tc.tile_pool(name="ring", bufs=4))
+        psum = ctx.enter_context(tc.psum_pool(name="psum", bufs=1))
+
+        def load_list(name, src):
+            tile = lists.tile([P, N // 16], U16, name=name)
+            nc.sync.dma_start(tile[:], src)
+            return tile
+
+        scale_table = keep.tile([P, T], U8, name="scale_table")
+        nc.vector.memset(scale_table[:].bitcast(I32), 0)
+        windows = [keep.tile([P, 2 * N], F32, name="window%d" % t) for t in range(PACK)]
+        for t in range(PACK):
+            nc.vector.memset(windows[t][:, N:], 0.0)
+        for q in range(4):
+            nc.scalar.dma_start(
+                scale_table[32 * q : 32 * q + 4, :].bitcast(I32),
+                x_scales[0, 4 * q : 4 * q + 4, :].bitcast(I32),
+            )
+
+        w1_raw = keep.tile([P, PACK, H], F32, name="w1_raw")
+        nc.sync.dma_start(w1_raw[:], w1.rearrange("(p j) c -> p j c", j=PACK))
+        offs_t = load_list("offs_t", offs)
+        two_t = load_list("two_t", two)
+        word_table = keep.tile([P, T], I32, name="word_table")
+        nc.sync.dma_start(word_table[:], x_words[0].rearrange("p n t -> p (n t)").bitcast(I32))
+        n2_t = load_list("n2_t", n2)
+        n1_t = load_list("n1_t", n1)
+        ga_t = keep.tile([P, PACK], F32, name="ga_t")
+        nc.sync.dma_start(ga_t[:], ga.rearrange("(p t) o -> p (t o)", t=PACK))
+        w2_raw = keep.tile([P, PACK, H], F32, name="w2_raw")
+        nc.sync.dma_start(w2_raw[:], w2.rearrange("(p j) c -> p j c", j=PACK))
+        gb_t = keep.tile([P, PACK], F32, name="gb_t")
+        nc.sync.dma_start(gb_t[:], gb.rearrange("(p t) o -> p (t o)", t=PACK))
+        n4_t = load_list("n4_t", n4)
+        n3_t = load_list("n3_t", n3)
+        n5_t = load_list("n5_t", n5)
+        n6_t = load_list("n6_t", n6)
+
+        def mx_tiles(name):
+            codes = keep.tile([P, N], U32, name=name + "_codes", align_bytes=64)
+            scales = keep.tile([P, N], U8, name=name + "_scales", align_bytes=64)
+            return codes, scales
+
+        def quantize(mx, grouped, c0, c1):
+            nc.vector.quantize_mx(
+                out=mx[0][:, c0:c1].bitcast(FP8X4),
+                scales=mx[1][:, c0:c1],
+                in_=grouped[:, PACK * c0 : PACK * c1],
+            )
+
+        def product(bank, lhs, t, rhs):
+            cols = slice(P * t, P * (t + 1))
+            nc.tensor.matmul_mx(
+                out=bank[:],
+                lhsT=lhs[0][:, cols].bitcast(FP8X4),
+                lhsT_scale=lhs[1][:, cols],
+                rhs=rhs[0][:].bitcast(FP8X4),
+                rhs_scale=rhs[1][:],
+                start=True,
+                stop=True,
+            )
+
+        def dealt_out(grouped):
+            return grouped[:].rearrange("p (u m j) -> p m j u", u=PACK, j=PACK)
+
+        def dealt_in(planes):
+            return planes[:].rearrange("p j (m u) -> p m j u", u=PACK)
+
+        xa = mx_tiles("xa")
+        xb = mx_tiles("xb")
+        w1_mx = mx_tiles("w1_mx")
+        w2_mx = mx_tiles("w2_mx")
+        z_mx = mx_tiles("z_mx")
+        z2_mx = mx_tiles("z2_mx")
+        banks_a = [psum.tile([P, N], F32, name="bank_a%d" % t) for t in range(PACK)]
+        banks_b = [psum.tile([P, N], F32, name="bank_b%d" % t) for t in range(PACK)]
+
+        nc.vector.tensor_copy(xa[1][:], scale_table[:].indirect(offs_t[:]))
+        w1_g = keep.tile([P, PACK * H], BF16, name="w1_g", align_bytes=64)
+        nc.vector.tensor_copy(dealt_out(w1_g), dealt_in(w1_raw))
+        nc.vector.tensor_copy(xb[1][:], scale_table[:].indirect(two_t[:]))
+        quantize(w1_mx, w1_g, 0, H)
+        nc.vector.tensor_copy(xa[0][:], word_table[:].bitcast(U32).indirect(offs_t[:]))
+        nc.vector.tensor_copy(xb[0][:], word_table[:].bitcast(U32).indirect(two_t[:]))
+
+        for t in range(PACK):
+            product(banks_a[t], w1_mx, t, xa)
+        for t in range(PACK):
+            nc.scalar.activation(windows[t][:, :N], banks_a[t][:], ACT.Copy)
+        w2_g = keep.tile([P, PACK * H], BF16, name="w2_g", align_bytes=64)
+        nc.scalar.activation(dealt_out(w2_g), dealt_in(w2_raw), ACT.Copy)
+        a_gain = keep.tile([P, PACK, N], F32, name="a_gain")
+        for t in range(PACK):
+            nc.scalar.activation(a_gain[:, t, :], banks_a[t][:], ACT.Copy, scale=ga_t[:, t : t + 1])
+
+        diff = keep.tile([P, PACK, N], F32, name="diff")
+        second = []
+        for t in range(PACK + 1):
+            if t < PACK:
+                g = ring.tile([P, N], F32, name="second")
+                nc.vector.tensor_copy(g[:], windows[t][:].indirect(n2_t[:]))
+                second.append(g)
+            if t > 0:
+                nc.vector.tensor_tensor(
+                    diff[:, t - 1, :], windows[t - 1][:].indirect(n1_t[:]), second[t - 1][:], ALU.subtract
+                )
+            if t == 2:
+                quantize(w2_mx, w2_g, 0, H)
+        for t in range(PACK):
+            product(banks_b[t], w2_mx, t, xb)
+        z_g = keep.tile([P, PACK * N], BF16, name="z_g", align_bytes=64)
+        nc.vector.tensor_tensor(dealt_out(z_g), dealt_in(diff), dealt_in(a_gain), ALU.mult)
+
+        b_tiles = [keep.tile([P, 2 * N], F32, name="b_tile%d" % t) for t in range(PACK)]
+        for t in range(PACK):
+            nc.scalar.activation(b_tiles[t][:, N:], banks_b[t][:], ACT.Copy)
+            nc.scalar.activation(windows[t][:, :N], banks_b[t][:], ACT.Tanh)
+            nc.scalar.activation(b_tiles[t][:, :N], banks_b[t][:], ACT.Copy, scale=gb_t[:, t : t + 1])
+        gated = []
+        for t in range(PACK):
+            g = ring.tile([P, N], F32, name="gated")
+            nc.vector.tensor_tensor(g[:], windows[t][:].indirect(n4_t[:]), b_tiles[t][:, N:], ALU.mult)
+            gated.append(g)
+            if t == 0:
+                quantize(z_mx, z_g, 0, N)
+        z2_g = keep.tile([P, PACK * N], BF16, name="z2_g", align_bytes=64)
+        cuts = [0, 256, 384, 512]
+        for s in range(3):
+            c0, c1 = cuts[s], cuts[s + 1]
+            z2_f = keep.tile([P, PACK, c1 - c0], F32, name="z2_f%d" % s)
+            for t in range(PACK):
+                nc.vector.tensor_tensor(
+                    z2_f[:, t, :],
+                    b_tiles[t][:].indirect(n3_t[:, c0 // 16 : c1 // 16]),
+                    gated[t][:, c0:c1],
+                    ALU.mult,
+                )
+            dst = z2_g[:, PACK * c0 : PACK * c1].rearrange("p (c i t) -> p c t i", i=4, t=PACK)
+            src = z2_f[:].rearrange("p t (c i) -> p c t i", i=4)
+            if s < 2:
+                nc.scalar.activation(dst, src, ACT.Copy)
+            else:
+                nc.vector.tensor_copy(dst, src)
+        for s in range(3):
+            quantize(z2_mx, z2_g, cuts[s], cuts[s + 1])
+
+        for t in range(PACK):
+            product(banks_a[t], z_mx, t, z2_mx)
+        inv = []
+        for t in range(PACK):
+            nc.scalar.activation(windows[t][:, :N], banks_a[t][:], ACT.Exp, scale=0.03125)
+            g = ring.tile([P, N], F32, name="inv")
+            nc.scalar.activation(g[:], banks_a[t][:], ACT.Exp, scale=-0.03125)
+            inv.append(g)
+        out_rows = out.rearrange("(p u) v -> p u v", u=PACK)
+        fifth, both = [], []
+        for t in range(PACK + 2):
+            if t < PACK:
+                g = ring.tile([P, N], F32, name="fifth")
+                nc.vector.tensor_copy(g[:], windows[t][:].indirect(n5_t[:]))
+                fifth.append(g)
+            if 1 <= t <= PACK:
+                g = ring.tile([P, N], F32, name="both")
+                nc.vector.tensor_tensor(g[:], windows[t - 1][:].indirect(n6_t[:]), fifth[t - 1][:], ALU.add)
+                both.append(g)
+            if t >= 2:
+                u = t - 2
+                ratio = ring.tile([P, N], F32, name="ratio")
+                nc.vector.tensor_tensor(ratio[:], both[u][:], inv[u][:], ALU.mult)
+                root = ring.tile([P, N], F32, name="root")
+                nc.scalar.activation(root[:], ratio[:], ACT.Abs_reciprocal_sqrt, bias=0.5, scale=0.5)
+                res = ring.tile([P, N], F32, name="res")
+                nc.scalar.activation(res[:], root[:], ACT.Square)
+                nc.sync.dma_start(out_rows[:, u, :], res[:])

@@ -27,7 +27,6 @@ def tile_picked_kqwindcubeshare_none_p_kernel(
     with ExitStack() as ctx:
         lists = ctx.enter_context(tc.tile_pool(name="lists", bufs=1))
         keep = ctx.enter_context(tc.tile_pool(name="keep", bufs=1))
-        ring = ctx.enter_context(tc.tile_pool(name="ring", bufs=4))
         psum = ctx.enter_context(tc.psum_pool(name="psum", bufs=1))
 
         def load_list(name, src):
@@ -36,7 +35,7 @@ def tile_picked_kqwindcubeshare_none_p_kernel(
             return tile
 
         scale_table = keep.tile([P, T], U8, name="scale_table")
-        nc.vector.memset(scale_table[:].bitcast(I32), 0)
+        nc.gpsimd.memset(scale_table[:].bitcast(I32), 0)
         windows = [keep.tile([P, 2 * N], F32, name="window%d" % t) for t in range(PACK)]
         for t in range(PACK):
             nc.vector.memset(windows[t][:, N:], 0.0)
@@ -46,22 +45,22 @@ def tile_picked_kqwindcubeshare_none_p_kernel(
                 x_scales[0, 4 * q : 4 * q + 4, :].bitcast(I32),
             )
 
-        w1_raw = keep.tile([P, PACK, H], F32, name="w1_raw")
-        nc.sync.dma_start(w1_raw[:], w1.rearrange("(p j) c -> p j c", j=PACK))
-        offs_t = load_list("offs_t", offs)
+        w2_raw = keep.tile([P, PACK, H], F32, name="w2_raw")
+        nc.sync.dma_start(w2_raw[:], w2.rearrange("(p j) c -> p j c", j=PACK))
         two_t = load_list("two_t", two)
         word_table = keep.tile([P, T], I32, name="word_table")
         nc.sync.dma_start(word_table[:], x_words[0].rearrange("p n t -> p (n t)").bitcast(I32))
-        n2_t = load_list("n2_t", n2)
-        n1_t = load_list("n1_t", n1)
-        ga_t = keep.tile([P, PACK], F32, name="ga_t")
-        nc.sync.dma_start(ga_t[:], ga.rearrange("(p t) o -> p (t o)", t=PACK))
-        w2_raw = keep.tile([P, PACK, H], F32, name="w2_raw")
-        nc.sync.dma_start(w2_raw[:], w2.rearrange("(p j) c -> p j c", j=PACK))
+        offs_t = load_list("offs_t", offs)
+        n4_t = load_list("n4_t", n4)
         gb_t = keep.tile([P, PACK], F32, name="gb_t")
         nc.sync.dma_start(gb_t[:], gb.rearrange("(p t) o -> p (t o)", t=PACK))
-        n4_t = load_list("n4_t", n4)
         n3_t = load_list("n3_t", n3)
+        w1_raw = keep.tile([P, PACK, H], F32, name="w1_raw")
+        nc.sync.dma_start(w1_raw[:], w1.rearrange("(p j) c -> p j c", j=PACK))
+        ga_t = keep.tile([P, PACK], F32, name="ga_t")
+        nc.sync.dma_start(ga_t[:], ga.rearrange("(p t) o -> p (t o)", t=PACK))
+        n2_t = load_list("n2_t", n2)
+        n1_t = load_list("n1_t", n1)
         n5_t = load_list("n5_t", n5)
         n6_t = load_list("n6_t", n6)
 
@@ -77,14 +76,14 @@ def tile_picked_kqwindcubeshare_none_p_kernel(
                 in_=grouped[:, PACK * c0 : PACK * c1],
             )
 
-        def product(bank, lhs, t, rhs):
+        def product(bank, lhs, t, rhs, c0=0, c1=N):
             cols = slice(P * t, P * (t + 1))
             nc.tensor.matmul_mx(
-                out=bank[:],
+                out=bank[:, c0:c1],
                 lhsT=lhs[0][:, cols].bitcast(FP8X4),
                 lhsT_scale=lhs[1][:, cols],
-                rhs=rhs[0][:].bitcast(FP8X4),
-                rhs_scale=rhs[1][:],
+                rhs=rhs[0][:, c0:c1].bitcast(FP8X4),
+                rhs_scale=rhs[1][:, c0:c1],
                 start=True,
                 stop=True,
             )
@@ -104,100 +103,118 @@ def tile_picked_kqwindcubeshare_none_p_kernel(
         banks_a = [psum.tile([P, N], F32, name="bank_a%d" % t) for t in range(PACK)]
         banks_b = [psum.tile([P, N], F32, name="bank_b%d" % t) for t in range(PACK)]
 
-        nc.vector.tensor_copy(xa[1][:], scale_table[:].indirect(offs_t[:]))
-        w1_g = keep.tile([P, PACK * H], BF16, name="w1_g", align_bytes=64)
-        nc.vector.tensor_copy(dealt_out(w1_g), dealt_in(w1_raw))
+        last = PACK - 1
         nc.vector.tensor_copy(xb[1][:], scale_table[:].indirect(two_t[:]))
-        quantize(w1_mx, w1_g, 0, H)
-        nc.vector.tensor_copy(xa[0][:], word_table[:].bitcast(U32).indirect(offs_t[:]))
+        w2_g = keep.tile([P, PACK * H], BF16, name="w2_g", align_bytes=64)
+        nc.scalar.activation(dealt_out(w2_g)[:, :56], dealt_in(w2_raw)[:, :56], ACT.Copy)
+        nc.vector.tensor_copy(dealt_out(w2_g)[:, 56:], dealt_in(w2_raw)[:, 56:])
+        quantize(w2_mx, w2_g, 0, H)
         nc.vector.tensor_copy(xb[0][:], word_table[:].bitcast(U32).indirect(two_t[:]))
+        nc.vector.tensor_copy(xa[1][:], scale_table[:].indirect(offs_t[:]))
+        nc.vector.tensor_copy(xa[0][:], word_table[:].bitcast(U32).indirect(offs_t[:]))
+
+        for t in range(PACK):
+            product(banks_b[t], w2_mx, t, xb)
+        b_tiles = [keep.tile([P, 2 * N], F32, name="b_tile%d" % t) for t in range(PACK)]
+        gated = [keep.tile([P, N], F32, name="gated%d" % t) for t in range(PACK)]
+        w1_g = keep.tile([P, PACK * H], BF16, name="w1_g", align_bytes=64)
+        z2_f = keep.tile([P, PACK, N], F32, name="z2_f")
+        for t in range(PACK + 1):
+            if t == last:
+                nc.scalar.activation(dealt_out(w1_g), dealt_in(w1_raw), ACT.Copy)
+                quantize(w1_mx, w1_g, 0, H)
+            if t < PACK:
+                nc.scalar.activation(b_tiles[t][:, N:], banks_b[t][:], ACT.Copy)
+                nc.scalar.activation(windows[t][:, :N], banks_b[t][:], ACT.Tanh)
+                nc.vector.tensor_tensor(gated[t][:], windows[t][:].indirect(n4_t[:]), b_tiles[t][:, N:], ALU.mult)
+            if t > 0:
+                u = t - 1
+                nc.scalar.activation(b_tiles[u][:, :N], banks_b[u][:], ACT.Copy, scale=gb_t[:, u : u + 1])
+                nc.vector.tensor_tensor(z2_f[:, u, :], b_tiles[u][:].indirect(n3_t[:]), gated[u][:], ALU.mult)
 
         for t in range(PACK):
             product(banks_a[t], w1_mx, t, xa)
         for t in range(PACK):
             nc.scalar.activation(windows[t][:, :N], banks_a[t][:], ACT.Copy)
-        w2_g = keep.tile([P, PACK * H], BF16, name="w2_g", align_bytes=64)
-        nc.scalar.activation(dealt_out(w2_g), dealt_in(w2_raw), ACT.Copy)
+        z2_g = keep.tile([P, PACK * N], BF16, name="z2_g", align_bytes=64)
+        nc.scalar.activation(
+            z2_g[:].rearrange("p (c i t) -> p c t i", i=4, t=PACK),
+            z2_f[:].rearrange("p t (c i) -> p c t i", i=4),
+            ACT.Copy,
+        )
         a_gain = keep.tile([P, PACK, N], F32, name="a_gain")
         for t in range(PACK):
             nc.scalar.activation(a_gain[:, t, :], banks_a[t][:], ACT.Copy, scale=ga_t[:, t : t + 1])
 
         diff = keep.tile([P, PACK, N], F32, name="diff")
-        second = []
+        first_fetch = keep.tile([P, N], F32, name="first_fetch")
+        fetched = [first_fetch[:]] + [windows[t][:, N:] for t in range(last)]
         for t in range(PACK + 1):
             if t < PACK:
-                g = ring.tile([P, N], F32, name="second")
-                nc.vector.tensor_copy(g[:], windows[t][:].indirect(n2_t[:]))
-                second.append(g)
+                nc.vector.tensor_copy(fetched[t], windows[t][:].indirect(n2_t[:]))
             if t > 0:
                 nc.vector.tensor_tensor(
-                    diff[:, t - 1, :], windows[t - 1][:].indirect(n1_t[:]), second[t - 1][:], ALU.subtract
+                    diff[:, t - 1, :], windows[t - 1][:].indirect(n1_t[:]), fetched[t - 1], ALU.subtract
                 )
-            if t == 2:
-                quantize(w2_mx, w2_g, 0, H)
-        for t in range(PACK):
-            product(banks_b[t], w2_mx, t, xb)
+        quantize(z2_mx, z2_g, 0, N)
         z_g = keep.tile([P, PACK * N], BF16, name="z_g", align_bytes=64)
-        nc.vector.tensor_tensor(dealt_out(z_g), dealt_in(diff), dealt_in(a_gain), ALU.mult)
-
-        b_tiles = [keep.tile([P, 2 * N], F32, name="b_tile%d" % t) for t in range(PACK)]
-        for t in range(PACK):
-            nc.scalar.activation(b_tiles[t][:, N:], banks_b[t][:], ACT.Copy)
-            nc.scalar.activation(windows[t][:, :N], banks_b[t][:], ACT.Tanh)
-            nc.scalar.activation(b_tiles[t][:, :N], banks_b[t][:], ACT.Copy, scale=gb_t[:, t : t + 1])
-        gated = []
-        for t in range(PACK):
-            g = ring.tile([P, N], F32, name="gated")
-            nc.vector.tensor_tensor(g[:], windows[t][:].indirect(n4_t[:]), b_tiles[t][:, N:], ALU.mult)
-            gated.append(g)
-            if t == 0:
-                quantize(z_mx, z_g, 0, N)
-        z2_g = keep.tile([P, PACK * N], BF16, name="z2_g", align_bytes=64)
-        cuts = [0, 256, 384, 512]
-        for s in range(3):
-            c0, c1 = cuts[s], cuts[s + 1]
-            z2_f = keep.tile([P, PACK, c1 - c0], F32, name="z2_f%d" % s)
-            for t in range(PACK):
+        for u in range(PACK + 1):
+            if u < PACK:
                 nc.vector.tensor_tensor(
-                    z2_f[:, t, :],
-                    b_tiles[t][:].indirect(n3_t[:, c0 // 16 : c1 // 16]),
-                    gated[t][:, c0:c1],
+                    z_g[:, N * u : N * (u + 1)].rearrange("p (m q t) -> p m t q", q=4, t=PACK),
+                    diff[:].rearrange("p t (m u q) -> p u m t q", u=PACK, q=4)[:, u],
+                    a_gain[:].rearrange("p t (m u q) -> p u m t q", u=PACK, q=4)[:, u],
                     ALU.mult,
                 )
-            dst = z2_g[:, PACK * c0 : PACK * c1].rearrange("p (c i t) -> p c t i", i=4, t=PACK)
-            src = z2_f[:].rearrange("p t (c i) -> p c t i", i=4)
-            if s < 2:
-                nc.scalar.activation(dst, src, ACT.Copy)
-            else:
-                nc.vector.tensor_copy(dst, src)
-        for s in range(3):
-            quantize(z2_mx, z2_g, cuts[s], cuts[s + 1])
+            if u > 0:
+                quantize(z_mx, z_g, P * (u - 1), P * u)
+                product(banks_b[u - 1], z_mx, u - 1, z2_mx)
+
+        inv = [keep.tile([P, N], F32, name="inv%d" % t) for t in range(PACK)]
+        both = [keep.tile([P, N], F32, name="both%d" % t) for t in range(PACK)]
+        ratio = [keep.tile([P, N], F32, name="ratio%d" % t) for t in range(PACK)]
+        root = [keep.tile([P, N], F32, name="root%d" % t) for t in range(PACK)]
+        res = keep.tile([P, PACK, N], F32, name="res")
+
+        def ex(t):
+            nc.scalar.activation(windows[t][:, :N], banks_b[t][:], ACT.Exp, scale=0.03125)
+
+        def ex_inv(t):
+            nc.scalar.activation(inv[t][:], banks_b[t][:], ACT.Exp, scale=-0.03125)
+
+        ex(0)
+        for t in range(1, PACK):
+            ex(t)
+            ex_inv(t - 1)
+        ex_inv(last)
+
+        out_rows = out.rearrange("(m u q) v -> q m u v", u=PACK, q=4)
+
+        def add_sixth(t, c0, c1):
+            nc.vector.tensor_tensor(
+                both[t][:, c0:c1], windows[t][:].indirect(n6_t[:, c0 // 16 : c1 // 16]), fetched[t][:, c0:c1], ALU.add
+            )
+
+        def finish(t, c0, c1):
+            nc.vector.tensor_tensor(ratio[t][:, c0:c1], both[t][:, c0:c1], inv[t][:, c0:c1], ALU.mult)
+            nc.scalar.activation(root[t][:, c0:c1], ratio[t][:, c0:c1], ACT.Abs_reciprocal_sqrt, bias=0.5, scale=0.5)
+            nc.scalar.activation(res[:, t, c0:c1], root[t][:, c0:c1], ACT.Square)
+
+        def store(t0, t1, queues):
+            for q in range(4):
+                queues[q % len(queues)].dma_start(out_rows[q, :, t0:t1, :], res[q:P:4, t0:t1, :])
 
         for t in range(PACK):
-            product(banks_a[t], z_mx, t, z2_mx)
-        inv = []
-        for t in range(PACK):
-            nc.scalar.activation(windows[t][:, :N], banks_a[t][:], ACT.Exp, scale=0.03125)
-            g = ring.tile([P, N], F32, name="inv")
-            nc.scalar.activation(g[:], banks_a[t][:], ACT.Exp, scale=-0.03125)
-            inv.append(g)
-        out_rows = out.rearrange("(p u) v -> p u v", u=PACK)
-        fifth, both = [], []
-        for t in range(PACK + 2):
-            if t < PACK:
-                g = ring.tile([P, N], F32, name="fifth")
-                nc.vector.tensor_copy(g[:], windows[t][:].indirect(n5_t[:]))
-                fifth.append(g)
-            if 1 <= t <= PACK:
-                g = ring.tile([P, N], F32, name="both")
-                nc.vector.tensor_tensor(g[:], windows[t - 1][:].indirect(n6_t[:]), fifth[t - 1][:], ALU.add)
-                both.append(g)
+            nc.vector.tensor_copy(fetched[t], windows[t][:].indirect(n5_t[:]))
+            if t >= 1:
+                add_sixth(t - 1, 0, N)
             if t >= 2:
-                u = t - 2
-                ratio = ring.tile([P, N], F32, name="ratio")
-                nc.vector.tensor_tensor(ratio[:], both[u][:], inv[u][:], ALU.mult)
-                root = ring.tile([P, N], F32, name="root")
-                nc.scalar.activation(root[:], ratio[:], ACT.Abs_reciprocal_sqrt, bias=0.5, scale=0.5)
-                res = ring.tile([P, N], F32, name="res")
-                nc.scalar.activation(res[:], root[:], ACT.Square)
-                nc.sync.dma_start(out_rows[:, u, :], res[:])
+                finish(t - 2, 0, N)
+        store(0, 2, [nc.sync])
+        add_sixth(last, 0, N // 2)
+        finish(last - 1, 0, N)
+        store(2, last, [nc.sync])
+        add_sixth(last, N // 2, N)
+        finish(last, 0, N // 2)
+        finish(last, N // 2, N)
+        store(last, PACK, [nc.sync, nc.scalar])

@@ -45,16 +45,16 @@ def tile_picked_kqwindcubeshare_none_p_kernel(
                 x_scales[0, 4 * q : 4 * q + 4, :].bitcast(I32),
             )
 
-        w2_raw = keep.tile([P, PACK, H], F32, name="w2_raw")
-        nc.sync.dma_start(w2_raw[:], w2.rearrange("(p j) c -> p j c", j=PACK))
         two_t = load_list("two_t", two)
-        word_table = keep.tile([P, T], I32, name="word_table")
-        nc.sync.dma_start(word_table[:], x_words[0].rearrange("p n t -> p (n t)").bitcast(I32))
         offs_t = load_list("offs_t", offs)
         n4_t = load_list("n4_t", n4)
+        n3_t = load_list("n3_t", n3)
+        w2_raw = keep.tile([P, PACK, H], F32, name="w2_raw")
+        nc.sync.dma_start(w2_raw[:], w2.rearrange("(p j) c -> p j c", j=PACK))
+        word_table = keep.tile([P, T], I32, name="word_table")
+        nc.sync.dma_start(word_table[:], x_words[0].rearrange("p n t -> p (n t)").bitcast(I32))
         gb_t = keep.tile([P, PACK], F32, name="gb_t")
         nc.sync.dma_start(gb_t[:], gb.rearrange("(p t) o -> p (t o)", t=PACK))
-        n3_t = load_list("n3_t", n3)
         w1_raw = keep.tile([P, PACK, H], F32, name="w1_raw")
         nc.sync.dma_start(w1_raw[:], w1.rearrange("(p j) c -> p j c", j=PACK))
         ga_t = keep.tile([P, PACK], F32, name="ga_t")
@@ -65,7 +65,7 @@ def tile_picked_kqwindcubeshare_none_p_kernel(
         n6_t = load_list("n6_t", n6)
 
         def mx_tiles(name):
-            codes = keep.tile([P, N], U32, name=name + "_codes", align_bytes=64)
+            codes = keep.tile([P, N], U32, name=name + "_codes", tag=name + "_codes", align_bytes=64)
             scales = keep.tile([P, N], U8, name=name + "_scales", align_bytes=64)
             return codes, scales
 
@@ -94,7 +94,6 @@ def tile_picked_kqwindcubeshare_none_p_kernel(
         def dealt_in(planes):
             return planes[:].rearrange("p j (m u) -> p m j u", u=PACK)
 
-        xa = mx_tiles("xa")
         xb = mx_tiles("xb")
         w1_mx = mx_tiles("w1_mx")
         w2_mx = mx_tiles("w2_mx")
@@ -104,23 +103,25 @@ def tile_picked_kqwindcubeshare_none_p_kernel(
         banks_b = [psum.tile([P, N], F32, name="bank_b%d" % t) for t in range(PACK)]
 
         last = PACK - 1
+        xa_scales = keep.tile([P, N], U8, name="xa_scales", align_bytes=64)
         nc.vector.tensor_copy(xb[1][:], scale_table[:].indirect(two_t[:]))
-        w2_g = keep.tile([P, PACK * H], BF16, name="w2_g", align_bytes=64)
-        nc.scalar.activation(dealt_out(w2_g)[:, :56], dealt_in(w2_raw)[:, :56], ACT.Copy)
-        nc.vector.tensor_copy(dealt_out(w2_g)[:, 56:], dealt_in(w2_raw)[:, 56:])
-        quantize(w2_mx, w2_g, 0, H)
+        nc.vector.tensor_copy(xa_scales[:], scale_table[:].indirect(offs_t[:]))
         nc.vector.tensor_copy(xb[0][:], word_table[:].bitcast(U32).indirect(two_t[:]))
-        nc.vector.tensor_copy(xa[1][:], scale_table[:].indirect(offs_t[:]))
-        nc.vector.tensor_copy(xa[0][:], word_table[:].bitcast(U32).indirect(offs_t[:]))
+        w2_g = keep.tile([P, PACK * H], BF16, name="w2_g", tag="w2_g_then_xa_codes", align_bytes=64)
+        nc.scalar.activation(dealt_out(w2_g), dealt_in(w2_raw), ACT.Copy)
+        quantize(w2_mx, w2_g, 0, H)
+        xa_codes = keep.tile([P, N], U32, name="xa_codes", tag="w2_g_then_xa_codes", align_bytes=64)
+        nc.vector.tensor_copy(xa_codes[:], word_table[:].bitcast(U32).indirect(offs_t[:]))
+        xa = (xa_codes, xa_scales)
 
         for t in range(PACK):
             product(banks_b[t], w2_mx, t, xb)
         b_tiles = [keep.tile([P, 2 * N], F32, name="b_tile%d" % t) for t in range(PACK)]
         gated = [keep.tile([P, N], F32, name="gated%d" % t) for t in range(PACK)]
-        w1_g = keep.tile([P, PACK * H], BF16, name="w1_g", align_bytes=64)
         z2_f = keep.tile([P, PACK, N], F32, name="z2_f")
         for t in range(PACK + 1):
             if t == last:
+                w1_g = keep.tile([P, PACK * H], BF16, name="w1_g", tag="w2_mx_codes", align_bytes=64)
                 nc.scalar.activation(dealt_out(w1_g), dealt_in(w1_raw), ACT.Copy)
                 quantize(w1_mx, w1_g, 0, H)
             if t < PACK:
@@ -146,16 +147,11 @@ def tile_picked_kqwindcubeshare_none_p_kernel(
         for t in range(PACK):
             nc.scalar.activation(a_gain[:, t, :], banks_a[t][:], ACT.Copy, scale=ga_t[:, t : t + 1])
 
-        diff = keep.tile([P, PACK, N], F32, name="diff")
-        first_fetch = keep.tile([P, N], F32, name="first_fetch")
-        fetched = [first_fetch[:]] + [windows[t][:, N:] for t in range(last)]
-        for t in range(PACK + 1):
-            if t < PACK:
-                nc.vector.tensor_copy(fetched[t], windows[t][:].indirect(n2_t[:]))
-            if t > 0:
-                nc.vector.tensor_tensor(
-                    diff[:, t - 1, :], windows[t - 1][:].indirect(n1_t[:]), fetched[t - 1], ALU.subtract
-                )
+        diff = z2_f
+        for t in range(PACK):
+            nc.vector.tensor_copy(gated[t][:], windows[t][:].indirect(n2_t[:]))
+        for t in range(PACK):
+            nc.vector.tensor_tensor(diff[:, t, :], windows[t][:].indirect(n1_t[:]), gated[t][:], ALU.subtract)
         quantize(z2_mx, z2_g, 0, N)
         z_g = keep.tile([P, PACK * N], BF16, name="z_g", align_bytes=64)
         for u in range(PACK + 1):
@@ -176,6 +172,8 @@ def tile_picked_kqwindcubeshare_none_p_kernel(
         root = [keep.tile([P, N], F32, name="root%d" % t) for t in range(PACK)]
         res = keep.tile([P, PACK, N], F32, name="res")
 
+        fifth = [g[:] for g in gated]
+
         def ex(t):
             nc.scalar.activation(windows[t][:, :N], banks_b[t][:], ACT.Exp, scale=0.03125)
 
@@ -183,38 +181,59 @@ def tile_picked_kqwindcubeshare_none_p_kernel(
             nc.scalar.activation(inv[t][:], banks_b[t][:], ACT.Exp, scale=-0.03125)
 
         ex(0)
-        for t in range(1, PACK):
-            ex(t)
-            ex_inv(t - 1)
-        ex_inv(last)
+        ex(1)
+        ex_inv(0)
+        ex(2)
+        nc.scalar.activation(b_tiles[last][:, :N], banks_b[last][:], ACT.Copy)
+        ex_inv(1)
+        nc.scalar.activation(fifth[last], b_tiles[last][:].indirect(n5_t[:]), ACT.Exp, scale=0.03125)
+        ex_inv(2)
+        ex(3)
+        ex_inv(3)
 
         out_rows = out.rearrange("(m u q) v -> q m u v", u=PACK, q=4)
 
         def add_sixth(t, c0, c1):
             nc.vector.tensor_tensor(
-                both[t][:, c0:c1], windows[t][:].indirect(n6_t[:, c0 // 16 : c1 // 16]), fetched[t][:, c0:c1], ALU.add
+                both[t][:, c0:c1], windows[t][:].indirect(n6_t[:, c0 // 16 : c1 // 16]), fifth[t][:, c0:c1], ALU.add
             )
 
-        def finish(t, c0, c1):
+        def take_root(t, c0, c1):
             nc.vector.tensor_tensor(ratio[t][:, c0:c1], both[t][:, c0:c1], inv[t][:, c0:c1], ALU.mult)
             nc.scalar.activation(root[t][:, c0:c1], ratio[t][:, c0:c1], ACT.Abs_reciprocal_sqrt, bias=0.5, scale=0.5)
-            nc.scalar.activation(res[:, t, c0:c1], root[t][:, c0:c1], ACT.Square)
+
+        def square(t, c0, c1):
+            if t < last:
+                nc.scalar.activation(res[:, t, c0:c1], root[t][:, c0:c1], ACT.Square)
+            else:
+                nc.vector.tensor_tensor(res[:, t, c0:c1], root[t][:, c0:c1], root[t][:, c0:c1], ALU.mult)
+
+        def finish(t, c0, c1):
+            take_root(t, c0, c1)
+            square(t, c0, c1)
 
         def store(t0, t1, queues):
             for q in range(4):
                 queues[q % len(queues)].dma_start(out_rows[q, :, t0:t1, :], res[q:P:4, t0:t1, :])
 
-        for t in range(PACK):
-            nc.vector.tensor_copy(fetched[t], windows[t][:].indirect(n5_t[:]))
-            if t >= 1:
-                add_sixth(t - 1, 0, N)
-            if t >= 2:
-                finish(t - 2, 0, N)
+        def fetch_fifth(t):
+            nc.vector.tensor_copy(fifth[t], windows[t][:].indirect(n5_t[:]))
+
+        fetch_fifth(0)
+        fetch_fifth(1)
+        add_sixth(0, 0, N)
+        fetch_fifth(2)
+        finish(0, 0, N)
+        add_sixth(1, 0, N)
+        add_sixth(2, 0, N)
+        finish(1, 0, N)
         store(0, 2, [nc.sync])
         add_sixth(last, 0, N // 2)
-        finish(last - 1, 0, N)
-        store(2, last, [nc.sync])
+        take_root(2, 0, N)
         add_sixth(last, N // 2, N)
-        finish(last, 0, N // 2)
-        finish(last, N // 2, N)
-        store(last, PACK, [nc.sync, nc.scalar])
+        take_root(last, 0, N // 2)
+        take_root(last, N // 2, N)
+        square(2, 0, N)
+        square(last, 0, N // 2)
+        square(last, N // 2, N)
+        store(2, PACK, [nc.sync, nc.scalar])

@@ -39,20 +39,20 @@ def tile_picked_kqwindcubeshare_none_p_kernel(
         windows = [keep.tile([P, 2 * N], F32, name="window%d" % t) for t in range(PACK)]
         for t in range(PACK):
             nc.vector.memset(windows[t][:, N:], 0.0)
+        scale_rows = keep.tile([P, T // 4], I32, name="scale_rows")
         for q in range(4):
-            nc.scalar.dma_start(
-                scale_table[32 * q : 32 * q + 4, :].bitcast(I32),
-                x_scales[0, 4 * q : 4 * q + 4, :].bitcast(I32),
-            )
+            nc.sync.dma_start(scale_rows[32 * q : 32 * q + 4, :], x_scales[0, 4 * q : 4 * q + 4, :].bitcast(I32))
+        for q in range(4):
+            nc.vector.tensor_copy(scale_table[32 * q : 32 * q + 4, :].bitcast(I32), scale_rows[32 * q : 32 * q + 4, :])
 
         two_t = load_list("two_t", two)
-        offs_t = load_list("offs_t", offs)
-        n4_t = load_list("n4_t", n4)
-        n3_t = load_list("n3_t", n3)
         w2_raw = keep.tile([P, PACK, H], F32, name="w2_raw")
         nc.sync.dma_start(w2_raw[:], w2.rearrange("(p j) c -> p j c", j=PACK))
         word_table = keep.tile([P, T], I32, name="word_table")
         nc.sync.dma_start(word_table[:], x_words[0].rearrange("p n t -> p (n t)").bitcast(I32))
+        offs_t = load_list("offs_t", offs)
+        n4_t = load_list("n4_t", n4)
+        n3_t = load_list("n3_t", n3)
         gb_t = keep.tile([P, PACK], F32, name="gb_t")
         nc.sync.dma_start(gb_t[:], gb.rearrange("(p t) o -> p (t o)", t=PACK))
         w1_raw = keep.tile([P, PACK, H], F32, name="w1_raw")
@@ -106,32 +106,40 @@ def tile_picked_kqwindcubeshare_none_p_kernel(
         xa_scales = keep.tile([P, N], U8, name="xa_scales", align_bytes=64)
         nc.vector.tensor_copy(xb[1][:], scale_table[:].indirect(two_t[:]))
         nc.vector.tensor_copy(xa_scales[:], scale_table[:].indirect(offs_t[:]))
-        nc.vector.tensor_copy(xb[0][:], word_table[:].bitcast(U32).indirect(two_t[:]))
         w2_g = keep.tile([P, PACK * H], BF16, name="w2_g", tag="w2_g_then_xa_codes", align_bytes=64)
-        nc.scalar.activation(dealt_out(w2_g), dealt_in(w2_raw), ACT.Copy)
+        nc.scalar.activation(dealt_out(w2_g)[:, :64], dealt_in(w2_raw)[:, :64], ACT.Copy)
+        nc.vector.tensor_copy(dealt_out(w2_g)[:, 64:], dealt_in(w2_raw)[:, 64:])
         quantize(w2_mx, w2_g, 0, H)
+        half = N // 2
+        for c0 in (0, half):
+            nc.vector.tensor_copy(
+                xb[0][:, c0 : c0 + half], word_table[:].bitcast(U32).indirect(two_t[:, c0 // 16 : (c0 + half) // 16])
+            )
         xa_codes = keep.tile([P, N], U32, name="xa_codes", tag="w2_g_then_xa_codes", align_bytes=64)
         nc.vector.tensor_copy(xa_codes[:], word_table[:].bitcast(U32).indirect(offs_t[:]))
         xa = (xa_codes, xa_scales)
 
+        b_parts = [[(banks_b[0], 0, half), (banks_a[0], half, N)]] + [[(banks_b[t], 0, N)] for t in range(1, PACK)]
         for t in range(PACK):
-            product(banks_b[t], w2_mx, t, xb)
+            for bank, c0, c1 in b_parts[t]:
+                product(bank, w2_mx, t, xb, c0, c1)
         b_tiles = [keep.tile([P, 2 * N], F32, name="b_tile%d" % t) for t in range(PACK)]
         gated = [keep.tile([P, N], F32, name="gated%d" % t) for t in range(PACK)]
         z2_f = keep.tile([P, PACK, N], F32, name="z2_f")
-        for t in range(PACK + 1):
-            if t == last:
+        for t in range(PACK):
+            for bank, c0, c1 in b_parts[t]:
+                nc.scalar.activation(b_tiles[t][:, N + c0 : N + c1], bank[:, c0:c1], ACT.Copy)
+                nc.scalar.activation(windows[t][:, c0:c1], bank[:, c0:c1], ACT.Tanh)
+            nc.vector.tensor_tensor(gated[t][:], windows[t][:].indirect(n4_t[:]), b_tiles[t][:, N:], ALU.mult)
+        for t in range(PACK):
+            if t == 2:
                 w1_g = keep.tile([P, PACK * H], BF16, name="w1_g", tag="w2_mx_codes", align_bytes=64)
-                nc.scalar.activation(dealt_out(w1_g), dealt_in(w1_raw), ACT.Copy)
+                nc.scalar.activation(dealt_out(w1_g)[:, :96], dealt_in(w1_raw)[:, :96], ACT.Copy)
+                nc.vector.tensor_copy(dealt_out(w1_g)[:, 96:], dealt_in(w1_raw)[:, 96:])
                 quantize(w1_mx, w1_g, 0, H)
-            if t < PACK:
-                nc.scalar.activation(b_tiles[t][:, N:], banks_b[t][:], ACT.Copy)
-                nc.scalar.activation(windows[t][:, :N], banks_b[t][:], ACT.Tanh)
-                nc.vector.tensor_tensor(gated[t][:], windows[t][:].indirect(n4_t[:]), b_tiles[t][:, N:], ALU.mult)
-            if t > 0:
-                u = t - 1
-                nc.scalar.activation(b_tiles[u][:, :N], banks_b[u][:], ACT.Copy, scale=gb_t[:, u : u + 1])
-                nc.vector.tensor_tensor(z2_f[:, u, :], b_tiles[u][:].indirect(n3_t[:]), gated[u][:], ALU.mult)
+            for bank, c0, c1 in b_parts[t]:
+                nc.scalar.activation(b_tiles[t][:, c0:c1], bank[:, c0:c1], ACT.Copy, scale=gb_t[:, t : t + 1])
+            nc.vector.tensor_tensor(z2_f[:, t, :], b_tiles[t][:].indirect(n3_t[:]), gated[t][:], ALU.mult)
 
         for t in range(PACK):
             product(banks_a[t], w1_mx, t, xa)

from contextlib import ExitStack

import concourse.mybir as mybir

K, T, S, V, H = 512, 2048, 512, 512, 512
FLOPS = 2 * K * H * S + 2 * K * H * V + 2 * H * S * V

F32 = mybir.dt.float32
BF16 = mybir.dt.bfloat16
I32 = mybir.dt.int32
U32 = mybir.dt.uint32
U16 = mybir.dt.uint16
U8 = mybir.dt.uint8
FP8X4 = mybir.dt.float8_e4m3fn_x4
ACT = mybir.ActivationFunctionType
ALU = mybir.AluOpType

P = 128
PACK = 4
N = 512


def tile_picked_kqwindcubeshare_none_p_kernel(
    tc, x_words, x_scales, w1, w2, ga, gb, offs, two, n1, n2, n3, n4, n5, n6, out
):
    nc = tc.nc
    with ExitStack() as ctx:
        lists = ctx.enter_context(tc.tile_pool(name="lists", bufs=1))
        keep = ctx.enter_context(tc.tile_pool(name="keep", bufs=1))
        psum = ctx.enter_context(tc.psum_pool(name="psum", bufs=1))

        def load_list(name, src):
            tile = lists.tile([P, N // 16], U16, name=name)
            nc.sync.dma_start(tile[:], src)
            return tile

        scale_table = keep.tile([P, T], U8, name="scale_table")
        nc.gpsimd.memset(scale_table[:].bitcast(I32), 0)
        windows = [keep.tile([P, 2 * N], F32, name="window%d" % t) for t in range(PACK)]
        for t in range(PACK):
            nc.vector.memset(windows[t][:, N:], 0.0)
        scale_rows = keep.tile([P, T // 4], I32, name="scale_rows")
        for q in range(4):
            nc.sync.dma_start(scale_rows[32 * q : 32 * q + 4, :], x_scales[0, 4 * q : 4 * q + 4, :].bitcast(I32))
        for q in range(4):
            nc.vector.tensor_copy(scale_table[32 * q : 32 * q + 4, :].bitcast(I32), scale_rows[32 * q : 32 * q + 4, :])

        two_t = load_list("two_t", two)
        w2_raw = keep.tile([P, PACK, H], F32, name="w2_raw")
        nc.sync.dma_start(w2_raw[:], w2.rearrange("(p j) c -> p j c", j=PACK))
        word_table = keep.tile([P, T], I32, name="word_table")
        nc.sync.dma_start(word_table[:], x_words[0].rearrange("p n t -> p (n t)").bitcast(I32))
        offs_t = load_list("offs_t", offs)
        n4_t = load_list("n4_t", n4)
        n3_t = load_list("n3_t", n3)
        gb_t = keep.tile([P, PACK], F32, name="gb_t")
        nc.sync.dma_start(gb_t[:], gb.rearrange("(p t) o -> p (t o)", t=PACK))
        w1_raw = keep.tile([P, PACK, H], F32, name="w1_raw")
        nc.sync.dma_start(w1_raw[:], w1.rearrange("(p j) c -> p j c", j=PACK))
        ga_t = keep.tile([P, PACK], F32, name="ga_t")
        nc.sync.dma_start(ga_t[:], ga.rearrange("(p t) o -> p (t o)", t=PACK))
        n2_t = load_list("n2_t", n2)
        n1_t = load_list("n1_t", n1)
        n5_t = load_list("n5_t", n5)
        n6_t = load_list("n6_t", n6)

        def mx_tiles(name):
            codes = keep.tile([P, N], U32, name=name + "_codes", tag=name + "_codes", align_bytes=64)
            scales = keep.tile([P, N], U8, name=name + "_scales", align_bytes=64)
            return codes, scales

        def quantize(mx, grouped, c0, c1):
            nc.vector.quantize_mx(
                out=mx[0][:, c0:c1].bitcast(FP8X4),
                scales=mx[1][:, c0:c1],
                in_=grouped[:, PACK * c0 : PACK * c1],
            )

        def product(bank, lhs, t, rhs, c0=0, c1=N):
            cols = slice(P * t, P * (t + 1))
            nc.tensor.matmul_mx(
                out=bank[:, c0:c1],
                lhsT=lhs[0][:, cols].bitcast(FP8X4),
                lhsT_scale=lhs[1][:, cols],
                rhs=rhs[0][:, c0:c1].bitcast(FP8X4),
                rhs_scale=rhs[1][:, c0:c1],
                start=True,
                stop=True,
            )

        def dealt_out(grouped):
            return grouped[:].rearrange("p (u m j) -> p m j u", u=PACK, j=PACK)

        def dealt_in(planes):
            return planes[:].rearrange("p j (m u) -> p m j u", u=PACK)

        xb = mx_tiles("xb")
        w1_mx = mx_tiles("w1_mx")
        w2_mx = mx_tiles("w2_mx")
        z_mx = mx_tiles("z_mx")
        z2_mx = mx_tiles("z2_mx")
        banks_a = [psum.tile([P, N], F32, name="bank_a%d" % t) for t in range(PACK)]
        banks_b = [psum.tile([P, N], F32, name="bank_b%d" % t) for t in range(PACK)]

        last = PACK - 1
        xa_scales = keep.tile([P, N], U8, name="xa_scales", align_bytes=64)
        nc.vector.tensor_copy(xb[1][:], scale_table[:].indirect(two_t[:]))
        nc.vector.tensor_copy(xa_scales[:], scale_table[:].indirect(offs_t[:]))
        w2_g = keep.tile([P, PACK * H], BF16, name="w2_g", tag="w2_g_then_xa_codes", align_bytes=64)
        nc.scalar.activation(dealt_out(w2_g)[:, :64], dealt_in(w2_raw)[:, :64], ACT.Copy)
        nc.vector.tensor_copy(dealt_out(w2_g)[:, 64:], dealt_in(w2_raw)[:, 64:])
        quantize(w2_mx, w2_g, 0, H)
        half = N // 2
        for c0 in (0, half):
            nc.vector.tensor_copy(
                xb[0][:, c0 : c0 + half], word_table[:].bitcast(U32).indirect(two_t[:, c0 // 16 : (c0 + half) // 16])
            )
        xa_codes = keep.tile([P, N], U32, name="xa_codes", tag="w2_g_then_xa_codes", align_bytes=64)
        nc.vector.tensor_copy(xa_codes[:], word_table[:].bitcast(U32).indirect(offs_t[:]))
        xa = (xa_codes, xa_scales)

        b_parts = [[(banks_b[0], 0, half), (banks_a[0], half, N)]] + [[(banks_b[t], 0, N)] for t in range(1, PACK)]
        for t in range(PACK):
            for bank, c0, c1 in b_parts[t]:
                product(bank, w2_mx, t, xb, c0, c1)
        b_tiles = [keep.tile([P, 2 * N], F32, name="b_tile%d" % t) for t in range(PACK)]
        gated = [keep.tile([P, N], F32, name="gated%d" % t) for t in range(PACK)]
        z2_f = keep.tile([P, PACK, N], F32, name="z2_f")
        for t in range(PACK):
            for bank, c0, c1 in b_parts[t]:
                nc.scalar.activation(b_tiles[t][:, N + c0 : N + c1], bank[:, c0:c1], ACT.Copy)
                nc.scalar.activation(windows[t][:, c0:c1], bank[:, c0:c1], ACT.Tanh)
            nc.vector.tensor_tensor(gated[t][:], windows[t][:].indirect(n4_t[:]), b_tiles[t][:, N:], ALU.mult)
        for t in range(PACK):
            if t == 2:
                w1_g = keep.tile([P, PACK * H], BF16, name="w1_g", tag="w2_mx_codes", align_bytes=64)
                nc.scalar.activation(dealt_out(w1_g)[:, :96], dealt_in(w1_raw)[:, :96], ACT.Copy)
                nc.vector.tensor_copy(dealt_out(w1_g)[:, 96:], dealt_in(w1_raw)[:, 96:])
                quantize(w1_mx, w1_g, 0, H)
            for bank, c0, c1 in b_parts[t]:
                nc.scalar.activation(b_tiles[t][:, c0:c1], bank[:, c0:c1], ACT.Copy, scale=gb_t[:, t : t + 1])
            nc.vector.tensor_tensor(z2_f[:, t, :], b_tiles[t][:].indirect(n3_t[:]), gated[t][:], ALU.mult)

        for t in range(PACK):
            product(banks_a[t], w1_mx, t, xa)
        for t in range(PACK):
            nc.scalar.activation(windows[t][:, :N], banks_a[t][:], ACT.Copy)
        z2_g = keep.tile([P, PACK * N], BF16, name="z2_g", align_bytes=64)
        nc.scalar.activation(
            z2_g[:].rearrange("p (c i t) -> p c t i", i=4, t=PACK),
            z2_f[:].rearrange("p t (c i) -> p c t i", i=4),
            ACT.Copy,
        )
        a_gain = keep.tile([P, PACK, N], F32, name="a_gain")
        for t in range(PACK):
            nc.scalar.activation(a_gain[:, t, :], banks_a[t][:], ACT.Copy, scale=ga_t[:, t : t + 1])

        diff = z2_f
        for t in range(PACK):
            nc.vector.tensor_copy(gated[t][:], windows[t][:].indirect(n2_t[:]))
        for t in range(PACK):
            nc.vector.tensor_tensor(diff[:, t, :], windows[t][:].indirect(n1_t[:]), gated[t][:], ALU.subtract)
        quantize(z2_mx, z2_g, 0, N)
        z_g = keep.tile([P, PACK * N], BF16, name="z_g", align_bytes=64)
        for u in range(PACK + 1):
            if u < PACK:
                nc.vector.tensor_tensor(
                    z_g[:, N * u : N * (u + 1)].rearrange("p (m q t) -> p m t q", q=4, t=PACK),
                    diff[:].rearrange("p t (m u q) -> p u m t q", u=PACK, q=4)[:, u],
                    a_gain[:].rearrange("p t (m u q) -> p u m t q", u=PACK, q=4)[:, u],
                    ALU.mult,
                )
            if u > 0:
                quantize(z_mx, z_g, P * (u - 1), P * u)
                product(banks_b[u - 1], z_mx, u - 1, z2_mx)

        inv = [keep.tile([P, N], F32, name="inv%d" % t) for t in range(PACK)]
        both = [keep.tile([P, N], F32, name="both%d" % t) for t in range(PACK)]
        ratio = [keep.tile([P, N], F32, name="ratio%d" % t) for t in range(PACK)]
        root = [keep.tile([P, N], F32, name="root%d" % t) for t in range(PACK)]
        res = keep.tile([P, PACK, N], F32, name="res")

        fifth = [g[:] for g in gated]

        def ex(t):
            nc.scalar.activation(windows[t][:, :N], banks_b[t][:], ACT.Exp, scale=0.03125)

        def ex_inv(t):
            nc.scalar.activation(inv[t][:], banks_b[t][:], ACT.Exp, scale=-0.03125)

        ex(0)
        ex(1)
        ex_inv(0)
        ex(2)
        nc.scalar.activation(b_tiles[last][:, :N], banks_b[last][:], ACT.Copy)
        ex_inv(1)
        nc.scalar.activation(fifth[last], b_tiles[last][:].indirect(n5_t[:]), ACT.Exp, scale=0.03125)
        ex_inv(2)
        ex(3)
        ex_inv(3)

        out_rows = out.rearrange("(m u q) v -> q m u v", u=PACK, q=4)

        def add_sixth(t, c0, c1):
            nc.vector.tensor_tensor(
                both[t][:, c0:c1], windows[t][:].indirect(n6_t[:, c0 // 16 : c1 // 16]), fifth[t][:, c0:c1], ALU.add
            )

        def take_root(t, c0, c1):
            nc.vector.tensor_tensor(ratio[t][:, c0:c1], both[t][:, c0:c1], inv[t][:, c0:c1], ALU.mult)
            nc.scalar.activation(root[t][:, c0:c1], ratio[t][:, c0:c1], ACT.Abs_reciprocal_sqrt, bias=0.5, scale=0.5)

        def square(t, c0, c1):
            if t < last:
                nc.scalar.activation(res[:, t, c0:c1], root[t][:, c0:c1], ACT.Square)
            else:
                nc.vector.tensor_tensor(res[:, t, c0:c1], root[t][:, c0:c1], root[t][:, c0:c1], ALU.mult)

        def finish(t, c0, c1):
            take_root(t, c0, c1)
            square(t, c0, c1)

        def store(t0, t1, queues):
            for q in range(4):
                queues[q % len(queues)].dma_start(out_rows[q, :, t0:t1, :], res[q:P:4, t0:t1, :])

        def fetch_fifth(t):
            nc.vector.tensor_copy(fifth[t], windows[t][:].indirect(n5_t[:]))

        fetch_fifth(0)
        fetch_fifth(1)
        add_sixth(0, 0, N)
        fetch_fifth(2)
        finish(0, 0, N)
        add_sixth(1, 0, N)
        add_sixth(2, 0, N)
        finish(1, 0, N)
        store(0, 2, [nc.sync])
        add_sixth(last, 0, N // 2)
        take_root(2, 0, N)
        add_sixth(last, N // 2, N)
        take_root(last, 0, N // 2)
        take_root(last, N // 2, N)
        square(2, 0, N)
        square(last, 0, N // 2)
        square(last, N // 2, N)
        store(2, PACK, [nc.sync, nc.scalar])
